import numpy as np
import ml_dtypes


def mxq(x, axis, fmt="e4m3"):
    dtype, down = {"e4m3": (ml_dtypes.float8_e4m3fn, 7), "e5m2": (ml_dtypes.float8_e5m2, 14)}[fmt]
    v = np.moveaxis(np.asarray(x, np.float32).astype(ml_dtypes.bfloat16).astype(np.float64), axis, -1)
    blocks = v.reshape(v.shape[:-1] + (-1, 32))
    amax = np.abs(blocks).max(-1, keepdims=True)
    byte = np.maximum(np.where(amax > 0, np.frexp(amax)[1] - 1 + 127, 0) - down, 1)
    scale = np.exp2(byte - 127.0)
    codes = (blocks / scale).astype(np.float32).astype(dtype).astype(np.float64)
    return np.moveaxis((codes * scale).reshape(v.shape), -1, axis)


WIDE = False


def mx_kscale(k):
    if not WIDE:
        return np.ones(k)
    levels = np.array([10, -10, 5, -5, 0])
    if k % 512:
        return np.exp2(np.random.permutation(np.resize(levels, k // 32))).repeat(32)
    a = np.empty((k // 512, 16))
    for p in range(k // 512):
        a[p, :8] = np.random.permutation(np.resize(levels, 8))
        for g in range(8):
            far = levels[np.abs(levels - a[p, g]) >= 10]
            a[p, g + 8] = far[np.random.randint(len(far))]
    return np.exp2(a.ravel()).repeat(32)


def f64(x):
    return np.asarray(x).astype(np.float64)


def striped(idx):
    return np.tile(idx.reshape(-1, 16).T, (8, 1)).astype(np.uint16)


def unstriped(offs):
    return offs[:16].T.reshape(-1).astype(np.int64)


def striped8(idx):
    return np.concatenate([x.reshape(-1, 16).T for x in idx]).astype(np.uint16)


def runs(offs, k):
    lists = np.stack([offs[16 * r : 16 * r + 16].T.reshape(-1) for r in range(8)]).astype(np.int64)
    return lists[np.arange(k) % 512 // 64]


def pack_weight(w):
    k, n = w.shape
    w = f64(np.asarray(w, np.float32).astype(ml_dtypes.bfloat16)).reshape(k // 32, 32, n)
    amax = np.abs(w).max(1)
    byte = np.clip(np.where(amax > 0, np.frexp(amax)[1] - 1 + 127 - 7, 1), 1, 254)
    scaled = (w * np.exp2(127.0 - byte)[:, None, :]).reshape(k, n).astype(np.float32)
    words = np.ascontiguousarray(scaled.reshape(k // 512, 128, 4, n).transpose(0, 1, 3, 2)).astype(ml_dtypes.float8_e4m3fn).view(np.uint8)
    return words, np.ascontiguousarray(byte.astype(np.uint8).reshape(k // 512, 16, n))


def unpack_weight(words, scales):
    g, p, n, _ = words.shape
    vals = np.ascontiguousarray(words).view(ml_dtypes.float8_e4m3fn).astype(np.float64) * np.repeat(np.exp2(scales.astype(np.float64) - 127.0), 8, axis=1)[..., None]
    return vals.transpose(0, 1, 3, 2).reshape(g * 512, n)

def planes(y):
    n, m = y.shape
    v = y.astype(np.float32).astype(ml_dtypes.bfloat16).astype(np.float64).reshape(n // 32, 32, m)
    top = np.abs(v).max(1)
    byte = np.clip(np.where(top > 0, np.frexp(top)[1] - 1 + 127 - 7, 1), 1, 254)
    codes = (v * np.exp2(127.0 - byte)[:, None, :]).reshape(n, m).astype(np.float32).astype(ml_dtypes.float8_e4m3fn).view(np.uint8)
    words = codes.reshape(n // 512, 128, 4, m).transpose(0, 1, 3, 2)
    return np.ascontiguousarray(words), np.ascontiguousarray(byte.astype(np.uint8).reshape(n // 512, 16, m))


K, T, S, N, G, H = 512, 2048, 512, 512, 2048, 512


def setup_inputs():
    n = np.random.standard_normal
    s = mx_kscale(K)[:, None]
    u = mx_kscale(H)
    packed_xT = pack_weight(n((K, T)) * s)
    packed_dT = pack_weight(n((K, G)) / s)
    packed_w1 = pack_weight(n((H, N)) / np.sqrt(H) / u[:, None])
    return {
        "x_words": packed_xT[0],
        "x_scales": packed_xT[1],
        "d_words": packed_dT[0],
        "d_scales": packed_dT[1],
        "gn": (np.random.uniform(0.5, 1.5, (H, 1)) * u[:, None]).astype(np.float32),
        "w1_words": packed_w1[0],
        "w1_scales": packed_w1[1],
        "offs": striped(np.random.permutation(T)[:S]),
        "kidx": striped8(np.random.randint(0, G, (8, H))),
        "n1": striped8(np.stack([np.random.permutation(S) for _ in range(8)])),
        "n2": striped8(np.stack([np.random.permutation(S) for _ in range(8)])),
    }


def reference(x_words, x_scales, d_words, d_scales, gn, w1_words, w1_scales, offs, kidx, n1, n2):
    d_kidx = unpack_weight(d_words, d_scales)[np.arange(K)[:, None], runs(kidx, K)]
    xq = unpack_weight(x_words, x_scales)[:, unstriped(offs)]
    s = 0.0625 * (d_kidx.T @ xq)
    a = s[np.arange(H)[:, None], runs(n1, H)]
    b = s[np.arange(H)[:, None], runs(n2, H)]
    mu = 0.3125 * (s + a + b)
    z = f64(gn) * ((s - mu) / (np.sqrt(0.5 * ((a - mu) ** 2 + (b - mu) ** 2) + 0.1)))
    out_0 = unpack_weight(w1_words, w1_scales).T @ mxq(z, 0, "e4m3")
    return (out_0,) + planes(out_0)

@@ -1,0 +1,218 @@
+from contextlib import ExitStack
+
+import concourse.mybir as mybir
+
+F32 = mybir.dt.float32
+BF16 = mybir.dt.bfloat16
+I32 = mybir.dt.int32
+U32 = mybir.dt.uint32
+U16 = mybir.dt.uint16
+U8 = mybir.dt.uint8
+FP8X4 = mybir.dt.float8_e4m3fn_x4
+ALU = mybir.AluOpType
+ACT = mybir.ActivationFunctionType
+
+P = 128
+PACK = 4
+TABLE = 2048
+S = 512
+CHUNKS = (256, 128, 128)
+FLOPS = 2 * 2 * 512 * 512 * 512
+
+
+def tile_picked_scorestd_none_po_kernel(
+    tc, x_words, x_scales, d_words, d_scales, gn, w1_words, w1_scales, offs, kidx, n1, n2, out_0, out_1, out_2
+):
+    nc = tc.nc
+    with ExitStack() as ctx:
+        keep = ctx.enter_context(tc.tile_pool(name="keep", bufs=1))
+        psum_s = ctx.enter_context(tc.psum_pool(name="psum_s", bufs=1))
+        psum_o = ctx.enter_context(tc.psum_pool(name="psum_o", bufs=4))
+
+        def words_of(ap):
+            return ap[0].rearrange("p n t -> p (n t)").bitcast(I32)
+
+        kidx_t = keep.tile([P, S // 16], U16, name="kidx_t")
+        offs_t = keep.tile([P, S // 16], U16, name="offs_t")
+        n1_t = keep.tile([P, S // 16], U16, name="n1_t")
+        n2_t = keep.tile([P, S // 16], U16, name="n2_t")
+        d_tab_bytes = keep.tile([P, TABLE], U8, name="d_tab_bytes", align_bytes=64)
+        x_tab_bytes = keep.tile([P, TABLE], U8, name="x_tab_bytes", align_bytes=64)
+        d_tab = keep.tile([P, TABLE], I32, name="d_tab", align_bytes=64)
+        x_tab = keep.tile([P, TABLE], I32, name="x_tab", align_bytes=64)
+        w_raw = keep.tile([P, S], I32, name="w_raw", align_bytes=64)
+        w_raw_bytes = keep.tile([P, S], U8, name="w_raw_bytes", align_bytes=64)
+        d_plane = keep.tile([P, S], U8, name="d_plane", align_bytes=64)
+        gn_t = keep.tile([P, PACK], F32, name="gn_t")
+
+        nc.vector.memset(d_tab_bytes[:].bitcast(I32), 0)
+        nc.vector.memset(x_tab_bytes[:].bitcast(I32), 0)
+        nc.gpsimd.memset(w_raw_bytes[:].bitcast(I32), 0)
+        nc.gpsimd.memset(d_plane[:].bitcast(I32), 0)
+
+        nc.sync.dma_start(kidx_t[:], kidx)
+        nc.sync.dma_start(d_tab_bytes[0:P:8, :].bitcast(I32), d_scales[0].bitcast(I32))
+        nc.sync.dma_start(offs_t[:], offs)
+        for q in range(4):
+            nc.sync.dma_start(x_tab_bytes[32 * q : 32 * q + 4, :].bitcast(I32), x_scales[0, 4 * q : 4 * q + 4, :].bitcast(I32))
+        nc.sync.dma_start(d_tab[:], words_of(d_words))
+        nc.sync.dma_start(x_tab[:], words_of(x_words))
+        nc.sync.dma_start(gn_t[:], gn.rearrange("(p t) o -> p (t o)", t=PACK))
+        nc.sync.dma_start(n1_t[:], n1)
+        nc.sync.dma_start(n2_t[:], n2)
+        nc.sync.dma_start(w_raw[:], words_of(w1_words))
+        for q in range(4):
+            nc.gpsimd.dma_start(w_raw_bytes[32 * q : 32 * q + 4, :].bitcast(I32), w1_scales[0, 4 * q : 4 * q + 4, :].bitcast(I32))
+
+        d_got_bytes = keep.tile([P, S], U8, name="d_got_bytes", align_bytes=64)
+        d_dealt_bytes = keep.tile([P, S], U8, name="d_dealt_bytes", align_bytes=64)
+        x_plane = keep.tile([P, S], U8, name="x_plane", align_bytes=64)
+        d_got = keep.tile([P, S], U32, name="d_got", align_bytes=64)
+        d_codes = keep.tile([P, S], U32, name="d_codes", align_bytes=64)
+        x_codes = keep.tile([P, S], U32, name="x_codes", align_bytes=64)
+        w_codes = keep.tile([P, S], U32, name="w_codes", align_bytes=64)
+        w_plane = keep.tile([P, S], U8, name="w_plane", align_bytes=64)
+
+        def dealt(dst, src):
+            return dst[:].rearrange("p (t m) -> p t m", t=PACK), src.rearrange("p (m t) -> p t m", t=PACK)
+
+        nc.vector.tensor_copy(d_got_bytes[:], d_tab_bytes[:].indirect(kidx_t[:]))
+        nc.vector.tensor_copy(*dealt(d_dealt_bytes, d_got_bytes[:]))
+        for j in range(4):
+            nc.scalar.dma_start(d_plane[j:P:32, :].bitcast(I32), d_dealt_bytes[8 * j : P : 32, :].bitcast(I32))
+        nc.vector.tensor_copy(x_plane[:], x_tab_bytes[:].indirect(offs_t[:]))
+        nc.vector.tensor_copy(d_got[:], d_tab[:].bitcast(U32).indirect(kidx_t[:]))
+        nc.vector.tensor_copy(*dealt(d_codes, d_got[:]))
+        nc.vector.tensor_copy(x_codes[:], x_tab[:].bitcast(U32).indirect(offs_t[:]))
+        nc.gpsimd.tensor_copy(*dealt(w_plane, w_raw_bytes[:]))
+        nc.scalar.copy(*dealt(w_codes, w_raw[:].bitcast(U32)))
+
+        gain = keep.tile([P, PACK], F32, name="gain")
+        size = keep.tile([P, PACK], F32, name="size")
+        floor = keep.tile([P, PACK], F32, name="floor")
+        undo = keep.tile([P, PACK], F32, name="undo")
+        nc.vector.tensor_scalar(gain[:], gn_t[:], 11.0 / 256.0, None, ALU.mult)
+        nc.vector.scalar_tensor_tensor(size[:], gn_t[:], -1.0, gn_t[:], ALU.mult, ALU.max)
+        nc.vector.tensor_scalar(floor[:], size[:], 11.0 / 5.0, 2.0**-120, ALU.mult, ALU.max)
+        nc.vector.reciprocal(undo[:], floor[:])
+
+        rows = []
+        for t in range(PACK):
+            bank = psum_s.tile([P, S], F32, name=f"s_bank{t}")
+            cols = slice(t * P, (t + 1) * P)
+            nc.tensor.matmul_mx(
+                out=bank[:], lhsT=d_codes[:, cols].bitcast(FP8X4), lhsT_scale=d_plane[:, cols],
+                rhs=x_codes[:].bitcast(FP8X4), rhs_scale=x_plane[:], start=True, stop=True,
+            )
+            row = keep.tile([P, S], F32, name=f"row{t}")
+            if t == 1:
+                nc.vector.tensor_scalar(row[:], bank[:], gain[:, t : t + 1], None, ALU.mult)
+            else:
+                nc.scalar.activation(row[:], bank[:], ACT.Copy, scale=gain[:, t : t + 1])
+            rows.append(row)
+
+        o_codes = keep.tile([P, S], I32, name="o_codes", align_bytes=64)
+        o_plane = keep.tile([P, S], U8, name="o_plane", align_bytes=64)
+        out_rows = out_0.rearrange("(p t) j -> p t j", t=PACK)
+        out_words = out_1[0].rearrange("p n t -> p (n t)").bitcast(I32)
+
+        starts = [sum(CHUNKS[:c]) for c in range(len(CHUNKS))]
+        units = [(c, t) for c in range(len(CHUNKS)) for t in range(PACK)]
+        num = [keep.tile([P, PACK, w], F32, name=f"num{c}") for c, w in enumerate(CHUNKS)]
+        root = [keep.tile([P, PACK, w], F32, name=f"root{c}") for c, w in enumerate(CHUNKS)]
+        held = {}
+
+        def cols_of(c):
+            return slice(starts[c], starts[c] + CHUNKS[c])
+
+        def list_of(c):
+            return slice(starts[c] // 16, (starts[c] + CHUNKS[c]) // 16)
+
+        def fetch_a(c, t):
+            a = keep.tile([P, CHUNKS[c]], F32, name=f"a{c}_{t}")
+            nc.scalar.activation(a[:], rows[t][:].indirect(n1_t[:, list_of(c)]), ACT.Copy)
+            held["a", c, t] = a
+
+        def linear(c, t):
+            a = held["a", c, t]
+            e = keep.tile([P, CHUNKS[c]], F32, name=f"e{c}_{t}")
+            dp = keep.tile([P, 2, CHUNKS[c]], F32, name=f"dp{c}_{t}")
+            nc.vector.tensor_tensor(e[:], rows[t][:].indirect(n2_t[:, list_of(c)]), a[:], ALU.add)
+            held["e", c, t] = e
+            held["dp", c, t] = dp
+
+        def linear2(c, t):
+            a, e, dp = held["a", c, t], held["e", c, t], held["dp", c, t]
+            nc.vector.scalar_tensor_tensor(dp[:, 0, :], a[:], -2.0, e[:], ALU.mult, ALU.add)
+            nc.vector.scalar_tensor_tensor(dp[:, 1, :], e[:], 0.6, rows[t][:, cols_of(c)], ALU.mult, ALU.subtract)
+            nc.vector.scalar_tensor_tensor(num[c][:, t, :], e[:], -5.0 / 11.0, rows[t][:, cols_of(c)], ALU.mult, ALU.add)
+
+        def squares(c, t):
+            sq = keep.tile([P, 2, CHUNKS[c]], F32, name=f"sq{c}_{t}")
+            nc.scalar.activation(sq[:], held["dp", c, t][:], ACT.Square, scale=undo[:, t : t + 1])
+            held["sq", c, t] = sq
+
+        def spread(c, t):
+            sq = held["sq", c, t]
+            var = keep.tile([P, CHUNKS[c]], F32, name=f"var{c}_{t}")
+            nc.vector.scalar_tensor_tensor(var[:], sq[:, 0, :], 2.56, sq[:, 1, :], ALU.mult, ALU.add)
+            held["var", c, t] = var
+
+        def inverse_root(c, t):
+            nc.scalar.activation(root[c][:, t, :], held["var", c, t][:], ACT.Abs_reciprocal_sqrt, bias=0.1)
+
+        def make_z(c):
+            width = CHUNKS[c]
+            z = keep.tile([P, width * PACK], BF16, name=f"z{c}", align_bytes=64)
+            nc.vector.tensor_tensor(
+                z[:].rearrange("p (c i t) -> p c t i", i=4, t=PACK),
+                num[c][:].rearrange("p t (c i) -> p c t i", i=4),
+                root[c][:].rearrange("p t (c i) -> p c t i", i=4),
+                ALU.mult,
+            )
+            held["z", c] = z
+
+        def product(c):
+            width = CHUNKS[c]
+            z_codes = keep.tile([P, width], U32, name=f"z_codes{c}", align_bytes=64)
+            z_plane = keep.tile([P, width], U8, name=f"z_plane{c}", align_bytes=64)
+            nc.vector.quantize_mx(out=z_codes[:].bitcast(FP8X4), scales=z_plane[:], in_=held["z", c][:])
+            res = keep.tile([P, PACK, width], F32, name=f"res{c}")
+            per_bank = S // width
+            for u in range(0, PACK, per_bank):
+                bank = psum_o.tile([P, S], F32, name="o_bank")
+                for v in range(per_bank):
+                    m = slice((u + v) * P, (u + v + 1) * P)
+                    nc.tensor.matmul_mx(
+                        out=bank[:, v * width : (v + 1) * width], lhsT=w_codes[:, m].bitcast(FP8X4), lhsT_scale=w_plane[:, m],
+                        rhs=z_codes[:].bitcast(FP8X4), rhs_scale=z_plane[:], start=True, stop=True,
+                    )
+                nc.scalar.copy(res[:, u : u + per_bank, :].rearrange("p t j -> p (t j)"), bank[:])
+            nc.sync.dma_start(out_rows[:, :, cols_of(c)], res[:])
+            held["res", c] = res
+
+        def round_out(c):
+            res16 = keep.tile([P, CHUNKS[c] * PACK], BF16, name=f"res16_{c}", align_bytes=64)
+            nc.vector.tensor_copy(
+                res16[:].rearrange("p (c i t) -> p c t i", i=4, t=PACK),
+                held["res", c][:].rearrange("p t (c i) -> p c t i", i=4),
+            )
+            held["res16", c] = res16
+
+        def planes(c):
+            cols = cols_of(c)
+            nc.vector.quantize_mx(out=o_codes[:, cols].bitcast(FP8X4), scales=o_plane[:, cols], in_=held["res16", c][:])
+            nc.sync.dma_start(out_words[:, cols], o_codes[:, cols])
+
+        unit_stages = (fetch_a, linear, linear2, squares, spread, inverse_root)
+        chunk_stages = (make_z, product, None, round_out, planes)
+        for step in range(len(units) + len(unit_stages) + len(chunk_stages)):
+            for k, stage in reversed(list(enumerate(chunk_stages))):
+                u = step - len(unit_stages) - k
+                if stage is not None and 0 <= u < len(units) and units[u][1] == PACK - 1:
+                    stage(units[u][0])
+            for k, stage in reversed(list(enumerate(unit_stages))):
+                if 0 <= step - k < len(units):
+                    stage(*units[step - k])
+        for q in range(4):
+            nc.sync.dma_start(out_2[0, 4 * q : 4 * q + 4, :].bitcast(I32), o_plane[32 * q : 32 * q + 4, :].bitcast(I32))

@@ -1,6 +1,7 @@
 from contextlib import ExitStack
 
 import concourse.mybir as mybir
+from concourse.masks import make_identity
 
 F32 = mybir.dt.float32
 BF16 = mybir.dt.bfloat16
@@ -16,7 +17,7 @@ P = 128
 PACK = 4
 TABLE = 2048
 S = 512
-CHUNKS = (256, 128, 128)
+ON_VECTOR = {0: 0, 2: 3}
 FLOPS = 2 * 2 * 512 * 512 * 512
 
 
@@ -26,8 +27,7 @@ def tile_picked_scorestd_none_po_kernel(
     nc = tc.nc
     with ExitStack() as ctx:
         keep = ctx.enter_context(tc.tile_pool(name="keep", bufs=1))
-        psum_s = ctx.enter_context(tc.psum_pool(name="psum_s", bufs=1))
-        psum_o = ctx.enter_context(tc.psum_pool(name="psum_o", bufs=4))
+        psum = ctx.enter_context(tc.psum_pool(name="psum", bufs=8))
 
         def words_of(ap):
             return ap[0].rearrange("p n t -> p (n t)").bitcast(I32)
@@ -45,10 +45,10 @@ def tile_picked_scorestd_none_po_kernel(
         d_plane = keep.tile([P, S], U8, name="d_plane", align_bytes=64)
         gn_t = keep.tile([P, PACK], F32, name="gn_t")
 
-        nc.vector.memset(d_tab_bytes[:].bitcast(I32), 0)
+        nc.gpsimd.memset(d_tab_bytes[:].bitcast(I32), 0)
         nc.vector.memset(x_tab_bytes[:].bitcast(I32), 0)
-        nc.gpsimd.memset(w_raw_bytes[:].bitcast(I32), 0)
         nc.gpsimd.memset(d_plane[:].bitcast(I32), 0)
+        nc.gpsimd.memset(w_raw_bytes[:].bitcast(I32), 0)
 
         nc.sync.dma_start(kidx_t[:], kidx)
         nc.sync.dma_start(d_tab_bytes[0:P:8, :].bitcast(I32), d_scales[0].bitcast(I32))
@@ -62,14 +62,14 @@ def tile_picked_scorestd_none_po_kernel(
         nc.sync.dma_start(n2_t[:], n2)
         nc.sync.dma_start(w_raw[:], words_of(w1_words))
         for q in range(4):
-            nc.gpsimd.dma_start(w_raw_bytes[32 * q : 32 * q + 4, :].bitcast(I32), w1_scales[0, 4 * q : 4 * q + 4, :].bitcast(I32))
+            nc.sync.dma_start(w_raw_bytes[32 * q : 32 * q + 4, :].bitcast(I32), w1_scales[0, 4 * q : 4 * q + 4, :].bitcast(I32))
 
         d_got_bytes = keep.tile([P, S], U8, name="d_got_bytes", align_bytes=64)
         d_dealt_bytes = keep.tile([P, S], U8, name="d_dealt_bytes", align_bytes=64)
         x_plane = keep.tile([P, S], U8, name="x_plane", align_bytes=64)
         d_got = keep.tile([P, S], U32, name="d_got", align_bytes=64)
         d_codes = keep.tile([P, S], U32, name="d_codes", align_bytes=64)
-        x_codes = keep.tile([P, S], U32, name="x_codes", align_bytes=64)
+        x_codes = [keep.tile([P, S // 2], U32, name=f"x_codes{h}", align_bytes=64) for h in range(2)]
         w_codes = keep.tile([P, S], U32, name="w_codes", align_bytes=64)
         w_plane = keep.tile([P, S], U8, name="w_plane", align_bytes=64)
 
@@ -83,119 +83,116 @@ def tile_picked_scorestd_none_po_kernel(
         nc.vector.tensor_copy(x_plane[:], x_tab_bytes[:].indirect(offs_t[:]))
         nc.vector.tensor_copy(d_got[:], d_tab[:].bitcast(U32).indirect(kidx_t[:]))
         nc.vector.tensor_copy(*dealt(d_codes, d_got[:]))
-        nc.vector.tensor_copy(x_codes[:], x_tab[:].bitcast(U32).indirect(offs_t[:]))
-        nc.gpsimd.tensor_copy(*dealt(w_plane, w_raw_bytes[:]))
-        nc.scalar.copy(*dealt(w_codes, w_raw[:].bitcast(U32)))
+        for h in range(2):
+            nc.vector.tensor_copy(x_codes[h][:], x_tab[:].bitcast(U32).indirect(offs_t[:, 16 * h : 16 * h + 16]))
 
-        gain = keep.tile([P, PACK], F32, name="gain")
-        size = keep.tile([P, PACK], F32, name="size")
-        floor = keep.tile([P, PACK], F32, name="floor")
-        undo = keep.tile([P, PACK], F32, name="undo")
-        nc.vector.tensor_scalar(gain[:], gn_t[:], 11.0 / 256.0, None, ALU.mult)
-        nc.vector.scalar_tensor_tensor(size[:], gn_t[:], -1.0, gn_t[:], ALU.mult, ALU.max)
-        nc.vector.tensor_scalar(floor[:], size[:], 11.0 / 5.0, 2.0**-120, ALU.mult, ALU.max)
-        nc.vector.reciprocal(undo[:], floor[:])
+        ident = keep.tile([P, P], F32, name="ident")
+        make_identity(nc, ident[:])
+        gain_s = keep.tile([P, PACK], F32, name="gain_s")
+        gain_e = keep.tile([P, PACK], F32, name="gain_e")
+        nc.vector.tensor_scalar(gain_s[:], gn_t[:], 11.0 / 16.0, None, ALU.mult)
+        nc.vector.tensor_scalar(gain_e[:], gn_t[:], 25.0 / 48.0, None, ALU.mult)
 
-        rows = []
+        rows = [keep.tile([P, S], F32, name=f"row{t}") for t in range(PACK)]
         for t in range(PACK):
-            bank = psum_s.tile([P, S], F32, name=f"s_bank{t}")
-            cols = slice(t * P, (t + 1) * P)
-            nc.tensor.matmul_mx(
-                out=bank[:], lhsT=d_codes[:, cols].bitcast(FP8X4), lhsT_scale=d_plane[:, cols],
-                rhs=x_codes[:].bitcast(FP8X4), rhs_scale=x_plane[:], start=True, stop=True,
-            )
-            row = keep.tile([P, S], F32, name=f"row{t}")
-            if t == 1:
-                nc.vector.tensor_scalar(row[:], bank[:], gain[:, t : t + 1], None, ALU.mult)
-            else:
-                nc.scalar.activation(row[:], bank[:], ACT.Copy, scale=gain[:, t : t + 1])
-            rows.append(row)
+            for h in range(2):
+                bank = psum.tile([P, S], F32, name="bank")
+                cols = slice(t * P, (t + 1) * P)
+                half = slice(h * 2 * P, (h + 1) * 2 * P)
+                nc.tensor.matmul_mx(
+                    out=bank[:, 0 : 2 * P], lhsT=d_codes[:, cols].bitcast(FP8X4), lhsT_scale=d_plane[:, cols],
+                    rhs=x_codes[h][:].bitcast(FP8X4), rhs_scale=x_plane[:, half], start=True, stop=True,
+                )
+                nc.scalar.activation(rows[t][:, half], bank[:, 0 : 2 * P], ACT.Copy, scale=0.0625)
+
 
         o_codes = keep.tile([P, S], I32, name="o_codes", align_bytes=64)
         o_plane = keep.tile([P, S], U8, name="o_plane", align_bytes=64)
         out_rows = out_0.rearrange("(p t) j -> p t j", t=PACK)
         out_words = out_1[0].rearrange("p n t -> p (n t)").bitcast(I32)
-
-        starts = [sum(CHUNKS[:c]) for c in range(len(CHUNKS))]
-        units = [(c, t) for c in range(len(CHUNKS)) for t in range(PACK)]
-        num = [keep.tile([P, PACK, w], F32, name=f"num{c}") for c, w in enumerate(CHUNKS)]
-        root = [keep.tile([P, PACK, w], F32, name=f"root{c}") for c, w in enumerate(CHUNKS)]
         held = {}
 
         def cols_of(c):
-            return slice(starts[c], starts[c] + CHUNKS[c])
+            return slice(c * P, (c + 1) * P)
 
-        def list_of(c):
-            return slice(starts[c] // 16, (starts[c] + CHUNKS[c]) // 16)
+        def fetch(c):
+            lists = slice(c * P // 16, (c + 2) * P // 16)
+            for t in range(PACK):
+                a = keep.tile([P, 2 * P], F32, name=f"a{c}_{t}")
+                b = keep.tile([P, 2 * P], F32, name=f"b{c}_{t}")
+                if t != ON_VECTOR[c]:
+                    nc.scalar.activation(a[:], rows[t][:].indirect(n1_t[:, lists]), ACT.Copy, scale=-0.6)
+                else:
+                    nc.vector.tensor_scalar(a[:], rows[t][:].indirect(n1_t[:, lists]), -0.6, 0.0, ALU.mult, ALU.add)
+                nc.vector.tensor_scalar(b[:], rows[t][:].indirect(n2_t[:, lists]), 0.6, 0.0, ALU.mult, ALU.add)
+                e = keep.tile([P, 2 * P], F32, name=f"e{c}_{t}")
+                nc.vector.tensor_tensor(e[:], a[:], b[:], ALU.subtract)
+                for h in range(2):
+                    half = slice(h * P, (h + 1) * P)
+                    held["a", c + h, t], held["b", c + h, t], held["e", c + h, t] = a[:, half], b[:, half], e[:, half]
 
-        def fetch_a(c, t):
-            a = keep.tile([P, CHUNKS[c]], F32, name=f"a{c}_{t}")
-            nc.scalar.activation(a[:], rows[t][:].indirect(n1_t[:, list_of(c)]), ACT.Copy)
-            held["a", c, t] = a
+        def add_turned(bank, t, first, second):
+            nc.tensor.matmul(bank[:, cols_of(t)], first, ident[:], start=True, stop=False, is_transpose=True)
+            nc.tensor.matmul(bank[:, cols_of(t)], second, ident[:], start=False, stop=True, is_transpose=True)
 
-        def linear(c, t):
-            a = held["a", c, t]
-            e = keep.tile([P, CHUNKS[c]], F32, name=f"e{c}_{t}")
-            dp = keep.tile([P, 2, CHUNKS[c]], F32, name=f"dp{c}_{t}")
-            nc.vector.tensor_tensor(e[:], rows[t][:].indirect(n2_t[:, list_of(c)]), a[:], ALU.add)
-            held["e", c, t] = e
-            held["dp", c, t] = dp
+        def linear(c):
+            d_bank = psum.tile([P, S], F32, name="bank")
+            p_bank = psum.tile([P, S], F32, name="bank")
+            num = keep.tile([P, PACK, P], F32, name=f"num{c}")
+            for t in range(PACK):
+                add_turned(d_bank, t, held["a", c, t], held["b", c, t])
+            for t in range(PACK):
+                add_turned(p_bank, t, held["e", c, t], rows[t][:, cols_of(c)])
+                nc.vector.scalar_tensor_tensor(
+                    num[:, t, :], held["e", c, t], gain_e[:, t : t + 1], gained[t][:, cols_of(c)], ALU.mult, ALU.add
+                )
+            held["d", c], held["p", c], held["num", c] = d_bank, p_bank, num
 
-        def linear2(c, t):
-            a, e, dp = held["a", c, t], held["e", c, t], held["dp", c, t]
-            nc.vector.scalar_tensor_tensor(dp[:, 0, :], a[:], -2.0, e[:], ALU.mult, ALU.add)
-            nc.vector.scalar_tensor_tensor(dp[:, 1, :], e[:], 0.6, rows[t][:, cols_of(c)], ALU.mult, ALU.subtract)
-            nc.vector.scalar_tensor_tensor(num[c][:, t, :], e[:], -5.0 / 11.0, rows[t][:, cols_of(c)], ALU.mult, ALU.add)
+        def squares(c):
+            d2 = keep.tile([P, S], F32, name=f"d2_{c}")
+            p2 = keep.tile([P, S], F32, name=f"p2_{c}")
+            nc.scalar.activation(d2[:], held["d", c][:], ACT.Square, scale=0.5 / 0.6)
+            nc.scalar.activation(p2[:], held["p", c][:], ACT.Square, scale=0.3125)
+            held["d2", c], held["p2", c] = d2, p2
 
-        def squares(c, t):
-            sq = keep.tile([P, 2, CHUNKS[c]], F32, name=f"sq{c}_{t}")
-            nc.scalar.activation(sq[:], held["dp", c, t][:], ACT.Square, scale=undo[:, t : t + 1])
-            held["sq", c, t] = sq
-
-        def spread(c, t):
-            sq = held["sq", c, t]
-            var = keep.tile([P, CHUNKS[c]], F32, name=f"var{c}_{t}")
-            nc.vector.scalar_tensor_tensor(var[:], sq[:, 0, :], 2.56, sq[:, 1, :], ALU.mult, ALU.add)
-            held["var", c, t] = var
-
-        def inverse_root(c, t):
-            nc.scalar.activation(root[c][:, t, :], held["var", c, t][:], ACT.Abs_reciprocal_sqrt, bias=0.1)
+        def spread(c):
+            bank = psum.tile([P, S], F32, name="bank")
+            for t in range(PACK):
+                add_turned(bank, t, held["d2", c][:, cols_of(t)], held["p2", c][:, cols_of(t)])
+            root = keep.tile([P, S], F32, name=f"root{c}")
+            nc.scalar.activation(root[:], bank[:], ACT.Abs_reciprocal_sqrt, bias=0.1)
+            held["root", c] = root
 
         def make_z(c):
-            width = CHUNKS[c]
-            z = keep.tile([P, width * PACK], BF16, name=f"z{c}", align_bytes=64)
+            z = keep.tile([P, S], BF16, name=f"z{c}", align_bytes=64)
             nc.vector.tensor_tensor(
                 z[:].rearrange("p (c i t) -> p c t i", i=4, t=PACK),
-                num[c][:].rearrange("p t (c i) -> p c t i", i=4),
-                root[c][:].rearrange("p t (c i) -> p c t i", i=4),
+                held["num", c][:].rearrange("p t (c i) -> p c t i", i=4),
+                held["root", c][:].rearrange("p (t c i) -> p c t i", i=4, t=PACK),
                 ALU.mult,
             )
             held["z", c] = z
 
         def product(c):
-            width = CHUNKS[c]
-            z_codes = keep.tile([P, width], U32, name=f"z_codes{c}", align_bytes=64)
-            z_plane = keep.tile([P, width], U8, name=f"z_plane{c}", align_bytes=64)
+            z_codes = keep.tile([P, P], U32, name=f"z_codes{c}", align_bytes=64)
+            z_plane = keep.tile([P, P], U8, name=f"z_plane{c}", align_bytes=64)
             nc.vector.quantize_mx(out=z_codes[:].bitcast(FP8X4), scales=z_plane[:], in_=held["z", c][:])
-            res = keep.tile([P, PACK, width], F32, name=f"res{c}")
-            per_bank = S // width
-            for u in range(0, PACK, per_bank):
-                bank = psum_o.tile([P, S], F32, name="o_bank")
-                for v in range(per_bank):
-                    m = slice((u + v) * P, (u + v + 1) * P)
-                    nc.tensor.matmul_mx(
-                        out=bank[:, v * width : (v + 1) * width], lhsT=w_codes[:, m].bitcast(FP8X4), lhsT_scale=w_plane[:, m],
-                        rhs=z_codes[:].bitcast(FP8X4), rhs_scale=z_plane[:], start=True, stop=True,
-                    )
-                nc.scalar.copy(res[:, u : u + per_bank, :].rearrange("p t j -> p (t j)"), bank[:])
-            nc.sync.dma_start(out_rows[:, :, cols_of(c)], res[:])
+            res = keep.tile([P, S], F32, name=f"res{c}")
+            bank = psum.tile([P, S], F32, name="bank")
+            for t in range(PACK):
+                nc.tensor.matmul_mx(
+                    out=bank[:, cols_of(t)], lhsT=w_codes[:, cols_of(t)].bitcast(FP8X4), lhsT_scale=w_plane[:, cols_of(t)],
+                    rhs=z_codes[:].bitcast(FP8X4), rhs_scale=z_plane[:], start=True, stop=True,
+                )
+            nc.scalar.copy(res[:], bank[:])
+            nc.sync.dma_start(out_rows[:, :, cols_of(c)], res[:].rearrange("p (t j) -> p t j", t=PACK))
             held["res", c] = res
 
         def round_out(c):
-            res16 = keep.tile([P, CHUNKS[c] * PACK], BF16, name=f"res16_{c}", align_bytes=64)
+            res16 = keep.tile([P, S], BF16, name=f"res16_{c}", align_bytes=64)
             nc.vector.tensor_copy(
                 res16[:].rearrange("p (c i t) -> p c t i", i=4, t=PACK),
-                held["res", c][:].rearrange("p t (c i) -> p c t i", i=4),
+                held["res", c][:].rearrange("p (t c i) -> p c t i", i=4, t=PACK),
             )
             held["res16", c] = res16
 
@@ -204,15 +201,19 @@ def tile_picked_scorestd_none_po_kernel(
             nc.vector.quantize_mx(out=o_codes[:, cols].bitcast(FP8X4), scales=o_plane[:, cols], in_=held["res16", c][:])
             nc.sync.dma_start(out_words[:, cols], o_codes[:, cols])
 
-        unit_stages = (fetch_a, linear, linear2, squares, spread, inverse_root)
-        chunk_stages = (make_z, product, None, round_out, planes)
-        for step in range(len(units) + len(unit_stages) + len(chunk_stages)):
-            for k, stage in reversed(list(enumerate(chunk_stages))):
-                u = step - len(unit_stages) - k
-                if stage is not None and 0 <= u < len(units) and units[u][1] == PACK - 1:
-                    stage(units[u][0])
-            for k, stage in reversed(list(enumerate(unit_stages))):
-                if 0 <= step - k < len(units):
-                    stage(*units[step - k])
+        fetch(0)
+        fetch(2)
+        nc.vector.tensor_copy(*dealt(w_plane, w_raw_bytes[:]))
+        nc.scalar.copy(*dealt(w_codes, w_raw[:].bitcast(U32)))
+        gained = []
+        for t in range(PACK):
+            g = keep.tile([P, S], F32, name=f"gained{t}")
+            nc.vector.tensor_scalar(g[:], rows[t][:], gain_s[:, t : t + 1], None, ALU.mult)
+            gained.append(g)
+        stages = (linear, squares, spread, make_z, product, round_out, planes)
+        for step in range(PACK + len(stages)):
+            for k, stage in reversed(list(enumerate(stages))):
+                if 0 <= step - k < PACK:
+                    stage(step - k)
         for q in range(4):
             nc.sync.dma_start(out_2[0, 4 * q : 4 * q + 4, :].bitcast(I32), o_plane[32 * q : 32 * q + 4, :].bitcast(I32))

@@ -17,7 +17,7 @@ P = 128
 PACK = 4
 TABLE = 2048
 S = 512
-ON_VECTOR = {0: 0, 2: 3}
+DIRECT = 3
 FLOPS = 2 * 2 * 512 * 512 * 512
 
 
@@ -117,36 +117,51 @@ def tile_picked_scorestd_none_po_kernel(
 
         def fetch(c):
             lists = slice(c * P // 16, (c + 2) * P // 16)
+            a = keep.tile([P, PACK, 2 * P], F32, name=f"a{c}")
+            b = keep.tile([P, PACK, 2 * P], F32, name=f"b{c}")
+            e = keep.tile([P, PACK, 2 * P], F32, name=f"e{c}")
             for t in range(PACK):
-                a = keep.tile([P, 2 * P], F32, name=f"a{c}_{t}")
-                b = keep.tile([P, 2 * P], F32, name=f"b{c}_{t}")
-                if t != ON_VECTOR[c]:
-                    nc.scalar.activation(a[:], rows[t][:].indirect(n1_t[:, lists]), ACT.Copy, scale=-0.6)
+                if c == 0 and t == 0:
+                    nc.vector.tensor_scalar(a[:, t, :], rows[t][:].indirect(n1_t[:, lists]), -0.6, 0.0, ALU.mult, ALU.add)
                 else:
-                    nc.vector.tensor_scalar(a[:], rows[t][:].indirect(n1_t[:, lists]), -0.6, 0.0, ALU.mult, ALU.add)
-                nc.vector.tensor_scalar(b[:], rows[t][:].indirect(n2_t[:, lists]), 0.6, 0.0, ALU.mult, ALU.add)
-                e = keep.tile([P, 2 * P], F32, name=f"e{c}_{t}")
-                nc.vector.tensor_tensor(e[:], a[:], b[:], ALU.subtract)
-                for h in range(2):
-                    half = slice(h * P, (h + 1) * P)
-                    held["a", c + h, t], held["b", c + h, t], held["e", c + h, t] = a[:, half], b[:, half], e[:, half]
+                    nc.scalar.activation(a[:, t, :], rows[t][:].indirect(n1_t[:, lists]), ACT.Copy, scale=-0.6)
+                nc.vector.tensor_scalar(b[:, t, :], rows[t][:].indirect(n2_t[:, lists]), 0.6, 0.0, ALU.mult, ALU.add)
+                nc.vector.tensor_tensor(e[:, t, :], a[:, t, :], b[:, t, :], ALU.subtract)
+            for h in range(2):
+                held["a", c + h], held["b", c + h], held["e", c + h] = a[:, :, cols_of(h)], b[:, :, cols_of(h)], e[:, :, cols_of(h)]
+            held["e_pair", c] = e
+
+        def numerators(c):
+            num = keep.tile([P, PACK, 2 * P], F32, name=f"num{c}")
+            for t in range(PACK):
+                nc.vector.scalar_tensor_tensor(
+                    num[:, t, :], held["e_pair", c][:, t, :], gain_e[:, t : t + 1], gained[t][:, c * P : (c + 2) * P], ALU.mult, ALU.add
+                )
+            for h in range(2):
+                held["num", c + h] = num[:, :, cols_of(h)]
 
         def add_turned(bank, t, first, second):
             nc.tensor.matmul(bank[:, cols_of(t)], first, ident[:], start=True, stop=False, is_transpose=True)
             nc.tensor.matmul(bank[:, cols_of(t)], second, ident[:], start=False, stop=True, is_transpose=True)
 
         def linear(c):
-            d_bank = psum.tile([P, S], F32, name="bank")
-            p_bank = psum.tile([P, S], F32, name="bank")
-            num = keep.tile([P, PACK, P], F32, name=f"num{c}")
-            for t in range(PACK):
-                add_turned(d_bank, t, held["a", c, t], held["b", c, t])
-            for t in range(PACK):
-                add_turned(p_bank, t, held["e", c, t], rows[t][:, cols_of(c)])
-                nc.vector.scalar_tensor_tensor(
-                    num[:, t, :], held["e", c, t], gain_e[:, t : t + 1], gained[t][:, cols_of(c)], ALU.mult, ALU.add
-                )
-            held["d", c], held["p", c], held["num", c] = d_bank, p_bank, num
+            a, b, e = held["a", c], held["b", c], held["e", c]
+            if c == DIRECT:
+                d = keep.tile([P, S], F32, name="d_direct")
+                p = keep.tile([P, S], F32, name="p_direct")
+                nc.vector.tensor_tensor(d[:].rearrange("p (t j) -> p t j", t=PACK), a, b, ALU.add)
+                for t in range(PACK):
+                    nc.vector.tensor_tensor(p[:, cols_of(t)], e[:, t, :], rows[t][:, cols_of(c)], ALU.add)
+            else:
+                d = psum.tile([P, S], F32, name="bank")
+                p = psum.tile([P, S], F32, name="bank")
+                for t in range(PACK):
+                    add_turned(d, t, a[:, t, :], b[:, t, :])
+                for t in range(PACK):
+                    add_turned(p, t, e[:, t, :], rows[t][:, cols_of(c)])
+            held["d", c], held["p", c] = d, p
+            if c % 2 == 0:
+                numerators(c)
 
         def squares(c):
             d2 = keep.tile([P, S], F32, name=f"d2_{c}")
@@ -156,9 +171,13 @@ def tile_picked_scorestd_none_po_kernel(
             held["d2", c], held["p2", c] = d2, p2
 
         def spread(c):
-            bank = psum.tile([P, S], F32, name="bank")
-            for t in range(PACK):
-                add_turned(bank, t, held["d2", c][:, cols_of(t)], held["p2", c][:, cols_of(t)])
+            if c == DIRECT:
+                bank = keep.tile([P, S], F32, name="var_direct")
+                nc.vector.tensor_tensor(bank[:], held["d2", c][:], held["p2", c][:], ALU.add)
+            else:
+                bank = psum.tile([P, S], F32, name="bank")
+                for t in range(PACK):
+                    add_turned(bank, t, held["d2", c][:, cols_of(t)], held["p2", c][:, cols_of(t)])
             root = keep.tile([P, S], F32, name=f"root{c}")
             nc.scalar.activation(root[:], bank[:], ACT.Abs_reciprocal_sqrt, bias=0.1)
             held["root", c] = root
@@ -167,7 +186,7 @@ def tile_picked_scorestd_none_po_kernel(
             z = keep.tile([P, S], BF16, name=f"z{c}", align_bytes=64)
             nc.vector.tensor_tensor(
                 z[:].rearrange("p (c i t) -> p c t i", i=4, t=PACK),
-                held["num", c][:].rearrange("p t (c i) -> p c t i", i=4),
+                held["num", c].rearrange("p t (c i) -> p c t i", i=4),
                 held["root", c][:].rearrange("p (t c i) -> p c t i", i=4, t=PACK),
                 ALU.mult,
             )
@@ -216,4 +235,5 @@ def tile_picked_scorestd_none_po_kernel(
                 if 0 <= step - k < PACK:
                     stage(step - k)
         for q in range(4):
-            nc.sync.dma_start(out_2[0, 4 * q : 4 * q + 4, :].bitcast(I32), o_plane[32 * q : 32 * q + 4, :].bitcast(I32))
+            queue = nc.scalar if q % 2 else nc.sync
+            queue.dma_start(out_2[0, 4 * q : 4 * q + 4, :].bitcast(I32), o_plane[32 * q : 32 * q + 4, :].bitcast(I32))

@@ -76,13 +76,16 @@ def tile_picked_scorestd_none_po_kernel(
         def dealt(dst, src):
             return dst[:].rearrange("p (t m) -> p t m", t=PACK), src.rearrange("p (m t) -> p t m", t=PACK)
 
+        def dealt_words(dst, src):
+            return dst[:].rearrange("p (t m n) -> p m t n", t=PACK, n=4), src.rearrange("p (m n t) -> p m t n", t=PACK, n=4)
+
         nc.vector.tensor_copy(d_got_bytes[:], d_tab_bytes[:].indirect(kidx_t[:]))
         nc.vector.tensor_copy(*dealt(d_dealt_bytes, d_got_bytes[:]))
         for j in range(4):
             nc.scalar.dma_start(d_plane[j:P:32, :].bitcast(I32), d_dealt_bytes[8 * j : P : 32, :].bitcast(I32))
         nc.vector.tensor_copy(x_plane[:], x_tab_bytes[:].indirect(offs_t[:]))
         nc.vector.tensor_copy(d_got[:], d_tab[:].bitcast(U32).indirect(kidx_t[:]))
-        nc.vector.tensor_copy(*dealt(d_codes, d_got[:]))
+        nc.vector.tensor_copy(*dealt_words(d_codes, d_got[:]))
         for h in range(2):
             nc.vector.tensor_copy(x_codes[h][:], x_tab[:].bitcast(U32).indirect(offs_t[:, 16 * h : 16 * h + 16]))
 
@@ -185,9 +188,9 @@ def tile_picked_scorestd_none_po_kernel(
         def make_z(c):
             z = keep.tile([P, S], BF16, name=f"z{c}", align_bytes=64)
             nc.vector.tensor_tensor(
-                z[:].rearrange("p (c i t) -> p c t i", i=4, t=PACK),
-                held["num", c].rearrange("p t (c i) -> p c t i", i=4),
-                held["root", c][:].rearrange("p (t c i) -> p c t i", i=4, t=PACK),
+                z[:].rearrange("p (c i t) -> p c t i", i=2, t=PACK),
+                held["num", c].rearrange("p t (c i) -> p c t i", i=2),
+                held["root", c][:].rearrange("p (t c i) -> p c t i", i=2, t=PACK),
                 ALU.mult,
             )
             held["z", c] = z
@@ -210,8 +213,8 @@ def tile_picked_scorestd_none_po_kernel(
         def round_out(c):
             res16 = keep.tile([P, S], BF16, name=f"res16_{c}", align_bytes=64)
             nc.vector.tensor_copy(
-                res16[:].rearrange("p (c i t) -> p c t i", i=4, t=PACK),
-                held["res", c][:].rearrange("p (t c i) -> p c t i", i=4, t=PACK),
+                res16[:].rearrange("p (c i t) -> p c t i", i=2, t=PACK),
+                held["res", c][:].rearrange("p (t c i) -> p c t i", i=2, t=PACK),
             )
             held["res16", c] = res16
 
@@ -223,7 +226,7 @@ def tile_picked_scorestd_none_po_kernel(
         fetch(0)
         fetch(2)
         nc.vector.tensor_copy(*dealt(w_plane, w_raw_bytes[:]))
-        nc.scalar.copy(*dealt(w_codes, w_raw[:].bitcast(U32)))
+        nc.scalar.copy(*dealt_words(w_codes, w_raw[:].bitcast(U32)))
         gained = []
         for t in range(PACK):
             g = keep.tile([P, S], F32, name=f"gained{t}")

@@ -17,7 +17,14 @@ P = 128
 PACK = 4
 TABLE = 2048
 S = 512
-DIRECT = 3
+HALF = S // 2
+CHUNKS = S // P
+GROUP = 16
+QUADS = 4
+SHARE = 0.6
+DIRECT = CHUNKS - 1
+A_ON_VECTOR = (0, 0)
+B_ON_SCALAR_FROM = 2
 FLOPS = 2 * 2 * 512 * 512 * 512
 
 
@@ -32,10 +39,19 @@ def tile_picked_scorestd_none_po_kernel(
         def words_of(ap):
             return ap[0].rearrange("p n t -> p (n t)").bitcast(I32)
 
-        kidx_t = keep.tile([P, S // 16], U16, name="kidx_t")
-        offs_t = keep.tile([P, S // 16], U16, name="offs_t")
-        n1_t = keep.tile([P, S // 16], U16, name="n1_t")
-        n2_t = keep.tile([P, S // 16], U16, name="n2_t")
+        def live_rows(plane, q):
+            return plane[32 * q : 32 * q + 4, :].bitcast(I32)
+
+        def scale_rows(ap, q):
+            return ap[0, 4 * q : 4 * q + 4, :].bitcast(I32)
+
+        def block(n):
+            return slice(n * P, (n + 1) * P)
+
+        kidx_t = keep.tile([P, S // GROUP], U16, name="kidx_t")
+        offs_t = keep.tile([P, S // GROUP], U16, name="offs_t")
+        n1_t = keep.tile([P, S // GROUP], U16, name="n1_t")
+        n2_t = keep.tile([P, S // GROUP], U16, name="n2_t")
         d_tab_bytes = keep.tile([P, TABLE], U8, name="d_tab_bytes", align_bytes=64)
         x_tab_bytes = keep.tile([P, TABLE], U8, name="x_tab_bytes", align_bytes=64)
         d_tab = keep.tile([P, TABLE], I32, name="d_tab", align_bytes=64)
@@ -53,41 +69,42 @@ def tile_picked_scorestd_none_po_kernel(
         nc.sync.dma_start(kidx_t[:], kidx)
         nc.sync.dma_start(d_tab_bytes[0:P:8, :].bitcast(I32), d_scales[0].bitcast(I32))
         nc.sync.dma_start(offs_t[:], offs)
-        for q in range(4):
-            nc.sync.dma_start(x_tab_bytes[32 * q : 32 * q + 4, :].bitcast(I32), x_scales[0, 4 * q : 4 * q + 4, :].bitcast(I32))
+        for q in range(QUADS):
+            nc.sync.dma_start(live_rows(x_tab_bytes, q), scale_rows(x_scales, q))
         nc.sync.dma_start(d_tab[:], words_of(d_words))
         nc.sync.dma_start(x_tab[:], words_of(x_words))
         nc.sync.dma_start(gn_t[:], gn.rearrange("(p t) o -> p (t o)", t=PACK))
         nc.sync.dma_start(n1_t[:], n1)
         nc.sync.dma_start(n2_t[:], n2)
         nc.sync.dma_start(w_raw[:], words_of(w1_words))
-        for q in range(4):
-            nc.sync.dma_start(w_raw_bytes[32 * q : 32 * q + 4, :].bitcast(I32), w1_scales[0, 4 * q : 4 * q + 4, :].bitcast(I32))
+        for q in range(QUADS):
+            nc.sync.dma_start(live_rows(w_raw_bytes, q), scale_rows(w1_scales, q))
 
         d_got_bytes = keep.tile([P, S], U8, name="d_got_bytes", align_bytes=64)
         d_dealt_bytes = keep.tile([P, S], U8, name="d_dealt_bytes", align_bytes=64)
         x_plane = keep.tile([P, S], U8, name="x_plane", align_bytes=64)
         d_got = keep.tile([P, S], U32, name="d_got", align_bytes=64)
         d_codes = keep.tile([P, S], U32, name="d_codes", align_bytes=64)
-        x_codes = [keep.tile([P, S // 2], U32, name=f"x_codes{h}", align_bytes=64) for h in range(2)]
+        x_codes = [keep.tile([P, HALF], U32, name=f"x_codes{h}", align_bytes=64) for h in range(2)]
         w_codes = keep.tile([P, S], U32, name="w_codes", align_bytes=64)
         w_plane = keep.tile([P, S], U8, name="w_plane", align_bytes=64)
 
-        def dealt(dst, src):
+        def dealt_bytes(dst, src):
             return dst[:].rearrange("p (t m) -> p t m", t=PACK), src.rearrange("p (m t) -> p t m", t=PACK)
 
         def dealt_words(dst, src):
             return dst[:].rearrange("p (t m n) -> p m t n", t=PACK, n=4), src.rearrange("p (m n t) -> p m t n", t=PACK, n=4)
 
         nc.vector.tensor_copy(d_got_bytes[:], d_tab_bytes[:].indirect(kidx_t[:]))
-        nc.vector.tensor_copy(*dealt(d_dealt_bytes, d_got_bytes[:]))
+        nc.vector.tensor_copy(*dealt_bytes(d_dealt_bytes, d_got_bytes[:]))
         for j in range(4):
             nc.scalar.dma_start(d_plane[j:P:32, :].bitcast(I32), d_dealt_bytes[8 * j : P : 32, :].bitcast(I32))
         nc.vector.tensor_copy(x_plane[:], x_tab_bytes[:].indirect(offs_t[:]))
         nc.vector.tensor_copy(d_got[:], d_tab[:].bitcast(U32).indirect(kidx_t[:]))
         nc.vector.tensor_copy(*dealt_words(d_codes, d_got[:]))
         for h in range(2):
-            nc.vector.tensor_copy(x_codes[h][:], x_tab[:].bitcast(U32).indirect(offs_t[:, 16 * h : 16 * h + 16]))
+            entries = slice(h * HALF // GROUP, (h + 1) * HALF // GROUP)
+            nc.vector.tensor_copy(x_codes[h][:], x_tab[:].bitcast(U32).indirect(offs_t[:, entries]))
 
         ident = keep.tile([P, P], F32, name="ident")
         make_identity(nc, ident[:])
@@ -96,103 +113,107 @@ def tile_picked_scorestd_none_po_kernel(
         nc.vector.tensor_scalar(gain_s[:], gn_t[:], 11.0 / 16.0, None, ALU.mult)
         nc.vector.tensor_scalar(gain_e[:], gn_t[:], 25.0 / 48.0, None, ALU.mult)
 
+        warm = keep.tile([P, 1], F32, name="warm")
+        nc.scalar.activation(warm[:], ident[:, 0:1], ACT.Abs_reciprocal_sqrt, bias=0.1)
+
         rows = [keep.tile([P, S], F32, name=f"row{t}") for t in range(PACK)]
         for t in range(PACK):
             for h in range(2):
                 bank = psum.tile([P, S], F32, name="bank")
-                cols = slice(t * P, (t + 1) * P)
-                half = slice(h * 2 * P, (h + 1) * 2 * P)
+                half = slice(h * HALF, (h + 1) * HALF)
                 nc.tensor.matmul_mx(
-                    out=bank[:, 0 : 2 * P], lhsT=d_codes[:, cols].bitcast(FP8X4), lhsT_scale=d_plane[:, cols],
+                    out=bank[:, 0:HALF], lhsT=d_codes[:, block(t)].bitcast(FP8X4), lhsT_scale=d_plane[:, block(t)],
                     rhs=x_codes[h][:].bitcast(FP8X4), rhs_scale=x_plane[:, half], start=True, stop=True,
                 )
-                nc.scalar.activation(rows[t][:, half], bank[:, 0 : 2 * P], ACT.Copy, scale=0.0625)
-
+                nc.scalar.activation(rows[t][:, half], bank[:, 0:HALF], ACT.Copy, scale=0.0625)
 
         o_codes = keep.tile([P, S], I32, name="o_codes", align_bytes=64)
         o_plane = keep.tile([P, S], U8, name="o_plane", align_bytes=64)
         out_rows = out_0.rearrange("(p t) j -> p t j", t=PACK)
-        out_words = out_1[0].rearrange("p n t -> p (n t)").bitcast(I32)
+        out_words = words_of(out_1)
         held = {}
 
-        def cols_of(c):
-            return slice(c * P, (c + 1) * P)
+        def gather(on_scalar, dst, window, factor):
+            if on_scalar:
+                nc.scalar.activation(dst, window, ACT.Copy, scale=factor)
+            else:
+                nc.vector.tensor_scalar(dst, window, factor, 0.0, ALU.mult, ALU.add)
 
-        def fetch(c):
-            lists = slice(c * P // 16, (c + 2) * P // 16)
-            a = keep.tile([P, PACK, 2 * P], F32, name=f"a{c}")
-            b = keep.tile([P, PACK, 2 * P], F32, name=f"b{c}")
-            e = keep.tile([P, PACK, 2 * P], F32, name=f"e{c}")
+        def fetch(h):
+            entries = slice(h * HALF // GROUP, (h + 1) * HALF // GROUP)
+            a_neg = keep.tile([P, PACK, HALF], F32, name=f"a_neg{h}")
+            b_pos = keep.tile([P, PACK, HALF], F32, name=f"b_pos{h}")
+            e_neg = keep.tile([P, PACK, HALF], F32, name=f"e_neg{h}")
             for t in range(PACK):
-                if c == 0 and t == 0:
-                    nc.vector.tensor_scalar(a[:, t, :], rows[t][:].indirect(n1_t[:, lists]), -0.6, 0.0, ALU.mult, ALU.add)
-                else:
-                    nc.scalar.activation(a[:, t, :], rows[t][:].indirect(n1_t[:, lists]), ACT.Copy, scale=-0.6)
-                nc.vector.tensor_scalar(b[:, t, :], rows[t][:].indirect(n2_t[:, lists]), 0.6, 0.0, ALU.mult, ALU.add)
-                nc.vector.tensor_tensor(e[:, t, :], a[:, t, :], b[:, t, :], ALU.subtract)
-            for h in range(2):
-                held["a", c + h], held["b", c + h], held["e", c + h] = a[:, :, cols_of(h)], b[:, :, cols_of(h)], e[:, :, cols_of(h)]
-            held["e_pair", c] = e
+                gather((h, t) != A_ON_VECTOR, a_neg[:, t, :], rows[t][:].indirect(n1_t[:, entries]), -SHARE)
+                gather(h == 1 and t >= B_ON_SCALAR_FROM, b_pos[:, t, :], rows[t][:].indirect(n2_t[:, entries]), SHARE)
+                nc.vector.tensor_tensor(e_neg[:, t, :], a_neg[:, t, :], b_pos[:, t, :], ALU.subtract)
+            for u in range(2):
+                held["fetched", 2 * h + u] = a_neg[:, :, block(u)], b_pos[:, :, block(u)], e_neg[:, :, block(u)]
+            held["e_neg_half", h] = e_neg
 
-        def numerators(c):
-            num = keep.tile([P, PACK, 2 * P], F32, name=f"num{c}")
+        def numerators(h):
+            num = keep.tile([P, PACK, HALF], F32, name=f"num{h}")
             for t in range(PACK):
                 nc.vector.scalar_tensor_tensor(
-                    num[:, t, :], held["e_pair", c][:, t, :], gain_e[:, t : t + 1], gained[t][:, c * P : (c + 2) * P], ALU.mult, ALU.add
+                    num[:, t, :], held["e_neg_half", h][:, t, :], gain_e[:, t : t + 1],
+                    gained[t][:, h * HALF : (h + 1) * HALF], ALU.mult, ALU.add,
                 )
-            for h in range(2):
-                held["num", c + h] = num[:, :, cols_of(h)]
+            for u in range(2):
+                held["num", 2 * h + u] = num[:, :, block(u)]
 
         def add_turned(bank, t, first, second):
-            nc.tensor.matmul(bank[:, cols_of(t)], first, ident[:], start=True, stop=False, is_transpose=True)
-            nc.tensor.matmul(bank[:, cols_of(t)], second, ident[:], start=False, stop=True, is_transpose=True)
+            nc.tensor.matmul(bank[:, block(t)], first, ident[:], start=True, stop=False, is_transpose=True)
+            nc.tensor.matmul(bank[:, block(t)], second, ident[:], start=False, stop=True, is_transpose=True)
 
         def linear(c):
-            a, b, e = held["a", c], held["b", c], held["e", c]
+            a_neg, b_pos, e_neg = held["fetched", c]
             if c == DIRECT:
-                d = keep.tile([P, S], F32, name="d_direct")
-                p = keep.tile([P, S], F32, name="p_direct")
-                nc.vector.tensor_tensor(d[:].rearrange("p (t j) -> p t j", t=PACK), a, b, ALU.add)
+                diff = keep.tile([P, S], F32, name="diff_direct")
+                rest = keep.tile([P, S], F32, name="rest_direct")
+                nc.vector.tensor_tensor(diff[:].rearrange("p (t j) -> p t j", t=PACK), a_neg, b_pos, ALU.add)
                 for t in range(PACK):
-                    nc.vector.tensor_tensor(p[:, cols_of(t)], e[:, t, :], rows[t][:, cols_of(c)], ALU.add)
+                    nc.vector.tensor_tensor(rest[:, block(t)], e_neg[:, t, :], rows[t][:, block(c)], ALU.add)
             else:
-                d = psum.tile([P, S], F32, name="bank")
-                p = psum.tile([P, S], F32, name="bank")
+                diff = psum.tile([P, S], F32, name="bank")
+                rest = psum.tile([P, S], F32, name="bank")
                 for t in range(PACK):
-                    add_turned(d, t, a[:, t, :], b[:, t, :])
+                    add_turned(diff, t, a_neg[:, t, :], b_pos[:, t, :])
                 for t in range(PACK):
-                    add_turned(p, t, e[:, t, :], rows[t][:, cols_of(c)])
-            held["d", c], held["p", c] = d, p
+                    add_turned(rest, t, e_neg[:, t, :], rows[t][:, block(c)])
+            held["diff", c], held["rest", c] = diff, rest
             if c % 2 == 0:
-                numerators(c)
+                numerators(c // 2)
 
         def squares(c):
-            d2 = keep.tile([P, S], F32, name=f"d2_{c}")
-            p2 = keep.tile([P, S], F32, name=f"p2_{c}")
-            nc.scalar.activation(d2[:], held["d", c][:], ACT.Square, scale=0.5 / 0.6)
-            nc.scalar.activation(p2[:], held["p", c][:], ACT.Square, scale=0.3125)
-            held["d2", c], held["p2", c] = d2, p2
+            diff2 = keep.tile([P, S], F32, name=f"diff2_{c}")
+            rest2 = keep.tile([P, S], F32, name=f"rest2_{c}")
+            nc.scalar.activation(diff2[:], held["diff", c][:], ACT.Square, scale=0.5 / SHARE)
+            nc.scalar.activation(rest2[:], held["rest", c][:], ACT.Square, scale=0.3125)
+            held["diff2", c], held["rest2", c] = diff2, rest2
 
         def spread(c):
             if c == DIRECT:
-                bank = keep.tile([P, S], F32, name="var_direct")
-                nc.vector.tensor_tensor(bank[:], held["d2", c][:], held["p2", c][:], ALU.add)
+                var = keep.tile([P, S], F32, name="var_direct")
+                nc.vector.tensor_tensor(var[:], held["diff2", c][:], held["rest2", c][:], ALU.add)
             else:
-                bank = psum.tile([P, S], F32, name="bank")
+                var = psum.tile([P, S], F32, name="bank")
                 for t in range(PACK):
-                    add_turned(bank, t, held["d2", c][:, cols_of(t)], held["p2", c][:, cols_of(t)])
+                    add_turned(var, t, held["diff2", c][:, block(t)], held["rest2", c][:, block(t)])
             root = keep.tile([P, S], F32, name=f"root{c}")
-            nc.scalar.activation(root[:], bank[:], ACT.Abs_reciprocal_sqrt, bias=0.1)
+            nc.scalar.activation(root[:], var[:], ACT.Abs_reciprocal_sqrt, bias=0.1)
             held["root", c] = root
+
+        def side_by_side(tile):
+            return tile[:].rearrange("p (n i t) -> p n t i", i=2, t=PACK)
+
+        def by_tile(tile):
+            return tile[:].rearrange("p (t n i) -> p n t i", i=2, t=PACK)
 
         def make_z(c):
             z = keep.tile([P, S], BF16, name=f"z{c}", align_bytes=64)
-            nc.vector.tensor_tensor(
-                z[:].rearrange("p (c i t) -> p c t i", i=2, t=PACK),
-                held["num", c].rearrange("p t (c i) -> p c t i", i=2),
-                held["root", c][:].rearrange("p (t c i) -> p c t i", i=2, t=PACK),
-                ALU.mult,
-            )
+            num = held["num", c].rearrange("p t (n i) -> p n t i", i=2)
+            nc.vector.tensor_tensor(side_by_side(z), num, by_tile(held["root", c]), ALU.mult)
             held["z", c] = z
 
         def product(c):
@@ -203,40 +224,36 @@ def tile_picked_scorestd_none_po_kernel(
             bank = psum.tile([P, S], F32, name="bank")
             for t in range(PACK):
                 nc.tensor.matmul_mx(
-                    out=bank[:, cols_of(t)], lhsT=w_codes[:, cols_of(t)].bitcast(FP8X4), lhsT_scale=w_plane[:, cols_of(t)],
+                    out=bank[:, block(t)], lhsT=w_codes[:, block(t)].bitcast(FP8X4), lhsT_scale=w_plane[:, block(t)],
                     rhs=z_codes[:].bitcast(FP8X4), rhs_scale=z_plane[:], start=True, stop=True,
                 )
             nc.scalar.copy(res[:], bank[:])
-            nc.sync.dma_start(out_rows[:, :, cols_of(c)], res[:].rearrange("p (t j) -> p t j", t=PACK))
+            nc.sync.dma_start(out_rows[:, :, block(c)], res[:].rearrange("p (t j) -> p t j", t=PACK))
             held["res", c] = res
 
         def round_out(c):
             res16 = keep.tile([P, S], BF16, name=f"res16_{c}", align_bytes=64)
-            nc.vector.tensor_copy(
-                res16[:].rearrange("p (c i t) -> p c t i", i=2, t=PACK),
-                held["res", c][:].rearrange("p (t c i) -> p c t i", i=2, t=PACK),
-            )
+            nc.vector.tensor_copy(side_by_side(res16), by_tile(held["res", c]))
             held["res16", c] = res16
 
-        def planes(c):
-            cols = cols_of(c)
-            nc.vector.quantize_mx(out=o_codes[:, cols].bitcast(FP8X4), scales=o_plane[:, cols], in_=held["res16", c][:])
-            nc.sync.dma_start(out_words[:, cols], o_codes[:, cols])
+        def hand_on(c):
+            nc.vector.quantize_mx(out=o_codes[:, block(c)].bitcast(FP8X4), scales=o_plane[:, block(c)], in_=held["res16", c][:])
+            nc.sync.dma_start(out_words[:, block(c)], o_codes[:, block(c)])
 
         fetch(0)
-        fetch(2)
-        nc.vector.tensor_copy(*dealt(w_plane, w_raw_bytes[:]))
+        fetch(1)
+        nc.vector.tensor_copy(*dealt_bytes(w_plane, w_raw_bytes[:]))
         nc.scalar.copy(*dealt_words(w_codes, w_raw[:].bitcast(U32)))
         gained = []
         for t in range(PACK):
-            g = keep.tile([P, S], F32, name=f"gained{t}")
-            nc.vector.tensor_scalar(g[:], rows[t][:], gain_s[:, t : t + 1], None, ALU.mult)
-            gained.append(g)
-        stages = (linear, squares, spread, make_z, product, round_out, planes)
-        for step in range(PACK + len(stages)):
+            scaled = keep.tile([P, S], F32, name=f"gained{t}")
+            nc.vector.tensor_scalar(scaled[:], rows[t][:], gain_s[:, t : t + 1], None, ALU.mult)
+            gained.append(scaled)
+        stages = (linear, squares, spread, make_z, product, round_out, hand_on)
+        for step in range(CHUNKS + len(stages) - 1):
             for k, stage in reversed(list(enumerate(stages))):
-                if 0 <= step - k < PACK:
+                if 0 <= step - k < CHUNKS:
                     stage(step - k)
-        for q in range(4):
+        for q in range(QUADS):
             queue = nc.scalar if q % 2 else nc.sync
-            queue.dma_start(out_2[0, 4 * q : 4 * q + 4, :].bitcast(I32), o_plane[32 * q : 32 * q + 4, :].bitcast(I32))
+            queue.dma_start(scale_rows(out_2, q), live_rows(o_plane, q))

from contextlib import ExitStack

import concourse.mybir as mybir
from concourse.masks import make_identity

F32 = mybir.dt.float32
BF16 = mybir.dt.bfloat16
I32 = mybir.dt.int32
U32 = mybir.dt.uint32
U16 = mybir.dt.uint16
U8 = mybir.dt.uint8
FP8X4 = mybir.dt.float8_e4m3fn_x4
ALU = mybir.AluOpType
ACT = mybir.ActivationFunctionType

P = 128
PACK = 4
TABLE = 2048
S = 512
HALF = S // 2
CHUNKS = S // P
GROUP = 16
QUADS = 4
SHARE = 0.6
DIRECT = CHUNKS - 1
A_ON_VECTOR = (0, 0)
B_ON_SCALAR_FROM = 2
FLOPS = 2 * 2 * 512 * 512 * 512


def tile_picked_scorestd_none_po_kernel(
    tc, x_words, x_scales, d_words, d_scales, gn, w1_words, w1_scales, offs, kidx, n1, n2, out_0, out_1, out_2
):
    nc = tc.nc
    with ExitStack() as ctx:
        keep = ctx.enter_context(tc.tile_pool(name="keep", bufs=1))
        psum = ctx.enter_context(tc.psum_pool(name="psum", bufs=8))

        def words_of(ap):
            return ap[0].rearrange("p n t -> p (n t)").bitcast(I32)

        def live_rows(plane, q):
            return plane[32 * q : 32 * q + 4, :].bitcast(I32)

        def scale_rows(ap, q):
            return ap[0, 4 * q : 4 * q + 4, :].bitcast(I32)

        def block(n):
            return slice(n * P, (n + 1) * P)

        kidx_t = keep.tile([P, S // GROUP], U16, name="kidx_t")
        offs_t = keep.tile([P, S // GROUP], U16, name="offs_t")
        n1_t = keep.tile([P, S // GROUP], U16, name="n1_t")
        n2_t = keep.tile([P, S // GROUP], U16, name="n2_t")
        d_tab_bytes = keep.tile([P, TABLE], U8, name="d_tab_bytes", align_bytes=64)
        x_tab_bytes = keep.tile([P, TABLE], U8, name="x_tab_bytes", align_bytes=64)
        d_tab = keep.tile([P, TABLE], I32, name="d_tab", align_bytes=64)
        x_tab = keep.tile([P, TABLE], I32, name="x_tab", align_bytes=64)
        w_raw = keep.tile([P, S], I32, name="w_raw", align_bytes=64)
        w_raw_bytes = keep.tile([P, S], U8, name="w_raw_bytes", align_bytes=64)
        d_plane = keep.tile([P, S], U8, name="d_plane", align_bytes=64)
        gn_t = keep.tile([P, PACK], F32, name="gn_t")

        nc.gpsimd.memset(d_tab_bytes[:].bitcast(I32), 0)
        nc.vector.memset(x_tab_bytes[:].bitcast(I32), 0)
        nc.gpsimd.memset(d_plane[:].bitcast(I32), 0)
        nc.gpsimd.memset(w_raw_bytes[:].bitcast(I32), 0)

        nc.sync.dma_start(kidx_t[:], kidx)
        nc.sync.dma_start(d_tab_bytes[0:P:8, :].bitcast(I32), d_scales[0].bitcast(I32))
        nc.sync.dma_start(offs_t[:], offs)
        for q in range(QUADS):
            nc.sync.dma_start(live_rows(x_tab_bytes, q), scale_rows(x_scales, q))
        nc.sync.dma_start(d_tab[:], words_of(d_words))
        nc.sync.dma_start(x_tab[:], words_of(x_words))
        nc.sync.dma_start(gn_t[:], gn.rearrange("(p t) o -> p (t o)", t=PACK))
        nc.sync.dma_start(n1_t[:], n1)
        nc.sync.dma_start(n2_t[:], n2)
        nc.sync.dma_start(w_raw[:], words_of(w1_words))
        for q in range(QUADS):
            nc.sync.dma_start(live_rows(w_raw_bytes, q), scale_rows(w1_scales, q))

        d_got_bytes = keep.tile([P, S], U8, name="d_got_bytes", align_bytes=64)
        d_dealt_bytes = keep.tile([P, S], U8, name="d_dealt_bytes", align_bytes=64)
        x_plane = keep.tile([P, S], U8, name="x_plane", align_bytes=64)
        d_got = keep.tile([P, S], U32, name="d_got", align_bytes=64)
        d_codes = keep.tile([P, S], U32, name="d_codes", align_bytes=64)
        x_codes = [keep.tile([P, HALF], U32, name=f"x_codes{h}", align_bytes=64) for h in range(2)]
        w_codes = keep.tile([P, S], U32, name="w_codes", align_bytes=64)
        w_plane = keep.tile([P, S], U8, name="w_plane", align_bytes=64)

        def dealt_bytes(dst, src):
            return dst[:].rearrange("p (t m) -> p t m", t=PACK), src.rearrange("p (m t) -> p t m", t=PACK)

        def dealt_words(dst, src):
            return dst[:].rearrange("p (t m n) -> p m t n", t=PACK, n=4), src.rearrange("p (m n t) -> p m t n", t=PACK, n=4)

        nc.vector.tensor_copy(d_got_bytes[:], d_tab_bytes[:].indirect(kidx_t[:]))
        nc.vector.tensor_copy(*dealt_bytes(d_dealt_bytes, d_got_bytes[:]))
        for j in range(4):
            nc.scalar.dma_start(d_plane[j:P:32, :].bitcast(I32), d_dealt_bytes[8 * j : P : 32, :].bitcast(I32))
        nc.vector.tensor_copy(x_plane[:], x_tab_bytes[:].indirect(offs_t[:]))
        nc.vector.tensor_copy(d_got[:], d_tab[:].bitcast(U32).indirect(kidx_t[:]))
        nc.vector.tensor_copy(*dealt_words(d_codes, d_got[:]))
        for h in range(2):
            entries = slice(h * HALF // GROUP, (h + 1) * HALF // GROUP)
            nc.vector.tensor_copy(x_codes[h][:], x_tab[:].bitcast(U32).indirect(offs_t[:, entries]))

        ident = keep.tile([P, P], F32, name="ident")
        make_identity(nc, ident[:])
        gain_s = keep.tile([P, PACK], F32, name="gain_s")
        gain_e = keep.tile([P, PACK], F32, name="gain_e")
        nc.vector.tensor_scalar(gain_s[:], gn_t[:], 11.0 / 16.0, None, ALU.mult)
        nc.vector.tensor_scalar(gain_e[:], gn_t[:], 25.0 / 48.0, None, ALU.mult)

        warm = keep.tile([P, 1], F32, name="warm")
        nc.scalar.activation(warm[:], ident[:, 0:1], ACT.Abs_reciprocal_sqrt, bias=0.1)

        rows = [keep.tile([P, S], F32, name=f"row{t}") for t in range(PACK)]
        for t in range(PACK):
            for h in range(2):
                bank = psum.tile([P, S], F32, name="bank")
                half = slice(h * HALF, (h + 1) * HALF)
                nc.tensor.matmul_mx(
                    out=bank[:, 0:HALF], lhsT=d_codes[:, block(t)].bitcast(FP8X4), lhsT_scale=d_plane[:, block(t)],
                    rhs=x_codes[h][:].bitcast(FP8X4), rhs_scale=x_plane[:, half], start=True, stop=True,
                )
                nc.scalar.activation(rows[t][:, half], bank[:, 0:HALF], ACT.Copy, scale=0.0625)

        o_codes = keep.tile([P, S], I32, name="o_codes", align_bytes=64)
        o_plane = keep.tile([P, S], U8, name="o_plane", align_bytes=64)
        out_rows = out_0.rearrange("(p t) j -> p t j", t=PACK)
        out_words = words_of(out_1)
        held = {}

        def gather(on_scalar, dst, window, factor):
            if on_scalar:
                nc.scalar.activation(dst, window, ACT.Copy, scale=factor)
            else:
                nc.vector.tensor_scalar(dst, window, factor, 0.0, ALU.mult, ALU.add)

        def fetch(h):
            entries = slice(h * HALF // GROUP, (h + 1) * HALF // GROUP)
            a_neg = keep.tile([P, PACK, HALF], F32, name=f"a_neg{h}")
            b_pos = keep.tile([P, PACK, HALF], F32, name=f"b_pos{h}")
            e_neg = keep.tile([P, PACK, HALF], F32, name=f"e_neg{h}")
            for t in range(PACK):
                gather((h, t) != A_ON_VECTOR, a_neg[:, t, :], rows[t][:].indirect(n1_t[:, entries]), -SHARE)
                gather(h == 1 and t >= B_ON_SCALAR_FROM, b_pos[:, t, :], rows[t][:].indirect(n2_t[:, entries]), SHARE)
                nc.vector.tensor_tensor(e_neg[:, t, :], a_neg[:, t, :], b_pos[:, t, :], ALU.subtract)
            for u in range(2):
                held["fetched", 2 * h + u] = a_neg[:, :, block(u)], b_pos[:, :, block(u)], e_neg[:, :, block(u)]
            held["e_neg_half", h] = e_neg

        def numerators(h):
            num = keep.tile([P, PACK, HALF], F32, name=f"num{h}")
            for t in range(PACK):
                nc.vector.scalar_tensor_tensor(
                    num[:, t, :], held["e_neg_half", h][:, t, :], gain_e[:, t : t + 1],
                    gained[t][:, h * HALF : (h + 1) * HALF], ALU.mult, ALU.add,
                )
            for u in range(2):
                held["num", 2 * h + u] = num[:, :, block(u)]

        def add_turned(bank, t, first, second):
            nc.tensor.matmul(bank[:, block(t)], first, ident[:], start=True, stop=False, is_transpose=True)
            nc.tensor.matmul(bank[:, block(t)], second, ident[:], start=False, stop=True, is_transpose=True)

        def linear(c):
            a_neg, b_pos, e_neg = held["fetched", c]
            if c == DIRECT:
                diff = keep.tile([P, S], F32, name="diff_direct")
                rest = keep.tile([P, S], F32, name="rest_direct")
                nc.vector.tensor_tensor(diff[:].rearrange("p (t j) -> p t j", t=PACK), a_neg, b_pos, ALU.add)
                for t in range(PACK):
                    nc.vector.tensor_tensor(rest[:, block(t)], e_neg[:, t, :], rows[t][:, block(c)], ALU.add)
            else:
                diff = psum.tile([P, S], F32, name="bank")
                rest = psum.tile([P, S], F32, name="bank")
                for t in range(PACK):
                    add_turned(diff, t, a_neg[:, t, :], b_pos[:, t, :])
                for t in range(PACK):
                    add_turned(rest, t, e_neg[:, t, :], rows[t][:, block(c)])
            held["diff", c], held["rest", c] = diff, rest
            if c % 2 == 0:
                numerators(c // 2)

        def squares(c):
            diff2 = keep.tile([P, S], F32, name=f"diff2_{c}")
            rest2 = keep.tile([P, S], F32, name=f"rest2_{c}")
            nc.scalar.activation(diff2[:], held["diff", c][:], ACT.Square, scale=0.5 / SHARE)
            nc.scalar.activation(rest2[:], held["rest", c][:], ACT.Square, scale=0.3125)
            held["diff2", c], held["rest2", c] = diff2, rest2

        def spread(c):
            if c == DIRECT:
                var = keep.tile([P, S], F32, name="var_direct")
                nc.vector.tensor_tensor(var[:], held["diff2", c][:], held["rest2", c][:], ALU.add)
            else:
                var = psum.tile([P, S], F32, name="bank")
                for t in range(PACK):
                    add_turned(var, t, held["diff2", c][:, block(t)], held["rest2", c][:, block(t)])
            root = keep.tile([P, S], F32, name=f"root{c}")
            nc.scalar.activation(root[:], var[:], ACT.Abs_reciprocal_sqrt, bias=0.1)
            held["root", c] = root

        def side_by_side(tile):
            return tile[:].rearrange("p (n i t) -> p n t i", i=2, t=PACK)

        def by_tile(tile):
            return tile[:].rearrange("p (t n i) -> p n t i", i=2, t=PACK)

        def make_z(c):
            z = keep.tile([P, S], BF16, name=f"z{c}", align_bytes=64)
            num = held["num", c].rearrange("p t (n i) -> p n t i", i=2)
            nc.vector.tensor_tensor(side_by_side(z), num, by_tile(held["root", c]), ALU.mult)
            held["z", c] = z

        def product(c):
            z_codes = keep.tile([P, P], U32, name=f"z_codes{c}", align_bytes=64)
            z_plane = keep.tile([P, P], U8, name=f"z_plane{c}", align_bytes=64)
            nc.vector.quantize_mx(out=z_codes[:].bitcast(FP8X4), scales=z_plane[:], in_=held["z", c][:])
            res = keep.tile([P, S], F32, name=f"res{c}")
            bank = psum.tile([P, S], F32, name="bank")
            for t in range(PACK):
                nc.tensor.matmul_mx(
                    out=bank[:, block(t)], lhsT=w_codes[:, block(t)].bitcast(FP8X4), lhsT_scale=w_plane[:, block(t)],
                    rhs=z_codes[:].bitcast(FP8X4), rhs_scale=z_plane[:], start=True, stop=True,
                )
            nc.scalar.copy(res[:], bank[:])
            nc.sync.dma_start(out_rows[:, :, block(c)], res[:].rearrange("p (t j) -> p t j", t=PACK))
            held["res", c] = res

        def round_out(c):
            res16 = keep.tile([P, S], BF16, name=f"res16_{c}", align_bytes=64)
            nc.vector.tensor_copy(side_by_side(res16), by_tile(held["res", c]))
            held["res16", c] = res16

        def hand_on(c):
            nc.vector.quantize_mx(out=o_codes[:, block(c)].bitcast(FP8X4), scales=o_plane[:, block(c)], in_=held["res16", c][:])
            nc.sync.dma_start(out_words[:, block(c)], o_codes[:, block(c)])

        fetch(0)
        fetch(1)
        nc.vector.tensor_copy(*dealt_bytes(w_plane, w_raw_bytes[:]))
        nc.scalar.copy(*dealt_words(w_codes, w_raw[:].bitcast(U32)))
        gained = []
        for t in range(PACK):
            scaled = keep.tile([P, S], F32, name=f"gained{t}")
            nc.vector.tensor_scalar(scaled[:], rows[t][:], gain_s[:, t : t + 1], None, ALU.mult)
            gained.append(scaled)
        stages = (linear, squares, spread, make_z, product, round_out, hand_on)
        for step in range(CHUNKS + len(stages) - 1):
            for k, stage in reversed(list(enumerate(stages))):
                if 0 <= step - k < CHUNKS:
                    stage(step - k)
        for q in range(QUADS):
            queue = nc.scalar if q % 2 else nc.sync
            queue.dma_start(scale_rows(out_2, q), live_rows(o_plane, q))
